import numpy as np
import ml_dtypes


def mxq(x, axis, fmt="e4m3"):
    dtype, down = {"e4m3": (ml_dtypes.float8_e4m3fn, 7), "e5m2": (ml_dtypes.float8_e5m2, 14)}[fmt]
    v = np.moveaxis(np.asarray(x, np.float32).astype(ml_dtypes.bfloat16).astype(np.float64), axis, -1)
    blocks = v.reshape(v.shape[:-1] + (-1, 32))
    amax = np.abs(blocks).max(-1, keepdims=True)
    byte = np.maximum(np.where(amax > 0, np.frexp(amax)[1] - 1 + 127, 0) - down, 1)
    scale = np.exp2(byte - 127.0)
    codes = (blocks / scale).astype(np.float32).astype(dtype).astype(np.float64)
    return np.moveaxis((codes * scale).reshape(v.shape), -1, axis)


WIDE = False


def mx_kscale(k):
    if not WIDE:
        return np.ones(k)
    levels = np.array([10, -10, 5, -5, 0])
    if k % 512:
        return np.exp2(np.random.permutation(np.resize(levels, k // 32))).repeat(32)
    a = np.empty((k // 512, 16))
    for p in range(k // 512):
        a[p, :8] = np.random.permutation(np.resize(levels, 8))
        for g in range(8):
            far = levels[np.abs(levels - a[p, g]) >= 10]
            a[p, g + 8] = far[np.random.randint(len(far))]
    return np.exp2(a.ravel()).repeat(32)


BF16 = ml_dtypes.bfloat16


def bf(x):
    return np.asarray(x, np.float32).astype(BF16)


def f64(x):
    return np.asarray(x).astype(np.float64)

def planes(Y):
    n, m = Y.shape
    b = f64(bf(Y)).reshape(n // 32, 32, m)
    amax = np.abs(b).max(1)
    byte = np.clip(np.where(amax > 0, np.frexp(amax)[1] - 1 + 127 - 7, 1), 1, 254)
    codes = (b * np.exp2(127.0 - byte)[:, None, :]).reshape(n, m).astype(np.float32).astype(ml_dtypes.float8_e4m3fn).view(np.uint8)
    words = codes.reshape(n // 512, 128, 4, m).transpose(0, 1, 3, 2)
    return np.ascontiguousarray(words), np.ascontiguousarray(byte.astype(np.uint8).reshape(n // 512, 16, m))


N, D, C = 1024, 1024, 1024
POSITIVE_THRESHOLD = 0.7
ALPHA_POSITIVE = 0.25
ALPHA_NEGATIVE = 0.75


def sigmoid(v):
    return 1.0 / (1.0 + np.exp(-v))


def softplus(v):
    return np.maximum(v, 0.0) + np.log1p(np.exp(-np.abs(v)))


def shift_scale_logits(r, t, a, b):
    sim = mxq(r, 1, "e4m3") @ mxq(t, 1, "e4m3").T
    return a[:, None] * (sim + b[:, None])


def labels_from_overlap(u):
    positive = u > POSITIVE_THRESHOLD
    s = np.where(positive, 1.0, -1.0)
    alpha = np.where(positive, ALPHA_POSITIVE, ALPHA_NEGATIVE)
    return s, alpha


def setup_inputs():
    fd, fn = mx_kscale(D), mx_kscale(N)
    return {
        "r": bf(np.random.standard_normal((N, D)) * fd[None, :] * fn[:, None]),
        "t": bf(np.random.standard_normal((C, D)) / np.sqrt(D) / fd[None, :]),
        "a": bf(np.random.uniform(0.5, 1.5, N) / fn),
        "b": bf(0.5 * np.random.standard_normal(N) * fn),
        "u": bf(np.random.uniform(0.0, 1.0, (N, C))),
    }


def core(r, t, a, b, u):
    r, t, a, b, u = f64(r), f64(t), f64(a), f64(b), f64(u)
    z = shift_scale_logits(r, t, a, b)
    s, alpha = labels_from_overlap(u)
    x = s * z
    p = sigmoid(x)
    lp = -softplus(-x)
    q = 1.0 - p
    e = a[:, None] * s * alpha * (q * q) * (2.0 * p * lp + p - 1.0)
    return (1.0 / 8.0) * (mxq(e, 0, "e4m3").T @ mxq(r, 0, "e4m3"))


def reference(r, t, a, b, u):
    R_out = core(r, t, a, b, u)
    words, scales = planes(R_out.T)
    return R_out, words, scales

@@ -1,0 +1,300 @@
+from contextlib import ExitStack
+
+import concourse.mybir as mybir
+from concourse.masks import make_identity
+
+N, D, C = 1024, 1024, 1024
+FLOPS = 2 * N * D * C * 2
+
+F32 = mybir.dt.float32
+BF16 = mybir.dt.bfloat16
+U32 = mybir.dt.uint32
+I32 = mybir.dt.int32
+U8 = mybir.dt.uint8
+FP8X4 = mybir.dt.float8_e4m3fn_x4
+ALU = mybir.AluOpType
+ACT = mybir.ActivationFunctionType
+
+P = 128
+BLOCKS = [(0, 256), (256, 256), (512, 256), (768, 128), (896, 128)]
+LOADS = "t0 t1 r0 r1 u0 t2 t3 r2 r3 u1"
+HEAD = "AB Tt,0,0,s Tt,0,1,v Tt,0,2,s Tt,0,3,v Tr,0,s Tr,1,v Tr,2,s Tr,3,s Qt,0,0 Qt,0,1 Qr,0 L,0,0,s L,0,1,s Qr,1 M,0,0 S,0,v V,0,0,0 V,0,0,1 V,0,0,2 V,0,0,3 Tt,1,0,s Tt,1,1,s Tt,1,2,s Tt,1,3,s Qn,0,0 Qn,0,1 W,0,0,g Qt,1,0 Qt,1,1 Tr,4,s Tr,5,s Tr,6,s Tr,7,s A,0,0,0 A,0,0,1 A,0,0,2 A,0,0,3 M,0,1 W,0,1,v V,0,1,0 V,0,1,1 S,1,v Qr,2 V,0,1,2 Qr,3 V,0,1,3 M,1,0 A,0,1,0 A,0,1,1 A,0,1,2 A,0,1,3 W,1,0,g W,1,1,g V,1,0,0 V,1,0,1 V,1,0,2 V,1,0,3 A,1,0,0 A,1,0,1 A,1,0,2 A,1,0,3 M,1,1 V,1,1,0 V,1,1,1 V,1,1,2 V,1,1,3 A,1,1,0 A,1,1,1 A,1,1,2 A,1,1,3 L,1,0,v L,1,1,v Qn,1,0 Qn,1,1"
+TAIL = "Ln,0,0 Ln,0,1 Sq,0,0 Sq,0,1 B,0,0 B,0,1 X,0,0 X,0,1 E,0,0 E,0,1 Qe,0,0 Qe,0,1 MP,0,0,0 MP,0,0,1 MR,0,0,0 MR,0,0,1 MP,0,1,0 MP,0,1,1 MR,0,1,0 MR,0,1,1 Ln,1,0 Ln,1,1 Sq,1,0 Sq,1,1 B,1,0 B,1,1 X,1,0 X,1,1 E,1,0 E,1,1 Qe,1,0 Qe,1,1 OP,0,0,0,s OP,0,0,1,s OR,0,0,0,s OR,0,0,1,v OP,0,1,0,s OP,0,1,1,s OR,0,1,0,s OR,0,1,1,s QP,0,0 QP,0,1 MP,1,0,0 MP,1,0,1 MR,1,0,0 MR,1,0,1 MP,1,1,0 MP,1,1,1 MR,1,1,0 MR,1,1,1 Ln,2,0 Ln,2,1 Sq,2,0 Sq,2,1 B,2,0 B,2,1 X,2,0 X,2,1 E,2,0 E,2,1 Qe,2,0 Qe,2,1 OP,1,0,0,s OP,1,0,1,s OR,1,0,0,s OR,1,0,1,v OP,1,1,0,s OP,1,1,1,s OR,1,1,0,s OR,1,1,1,s QP,1,0 QP,1,1 MP,2,0,0 MP,2,0,1 MR,2,0,0 MR,2,0,1 MP,2,1,0 MP,2,1,1 MR,2,1,0 MR,2,1,1 Ln,3,0 Ln,3,1 Sq,3,0 Sq,3,1 B,3,0 B,3,1 X,3,0 X,3,1 E,3,0 E,3,1 Qe,3,0 Qe,3,1 OP,2,0,0,s OP,2,0,1,s OR,2,0,0,s OR,2,0,1,v OP,2,1,0,s OP,2,1,1,s OR,2,1,0,s OR,2,1,1,s QP,2,0 QP,2,1 MP,3,0,0 MP,3,0,1 MR,3,0,0 MR,3,0,1 Ln,4,0 Ln,4,1 Sq,4,0 Sq,4,1 B,4,0 B,4,1 X,4,0 X,4,1 E,4,0 E,4,1 Qe,4,0 Qe,4,1 OP,3,0,0,s OP,3,0,1,s OR,3,0,0,s OR,3,0,1,v QP,3,0 QP,3,1 MP,4,0,0 MP,4,0,1 MR,4,0,0 MR,4,0,1 SC,0,896 OP,4,0,0,s OP,4,0,1,s OR,4,0,0,s OR,4,0,1,v QP,4,0 QP,4,1 SC,896,1024"
+
+
+def tile_owlshiftscalefocaltextgradient_x1_kernel(tc, r, t, a, b, u, out_0, out_1, out_2):
+    nc = tc.nc
+    with ExitStack() as ctx:
+        keep = ctx.enter_context(tc.tile_pool(name="keep", bufs=1))
+        big = ctx.enter_context(tc.tile_pool(name="big", bufs=4))
+        work = ctx.enter_context(tc.tile_pool(name="work", bufs=4))
+        psum = ctx.enter_context(tc.psum_pool(name="psum", bufs=8))
+        ctx.enter_context(tc.manual_schedule())
+
+        a_in = keep.tile([P, 8], BF16, name="a_in", align_bytes=64)
+        b_in = keep.tile([P, 8], BF16, name="b_in", align_bytes=64)
+        nc.scalar.dma_start(out=a_in[:].rearrange("p (g t) -> p g t", t=4), in_=a.rearrange("(g p t) -> p g t", p=P, t=4))
+        nc.scalar.dma_start(out=b_in[:].rearrange("p (g t) -> p g t", t=4), in_=b.rearrange("(g p t) -> p g t", p=P, t=4))
+        t_in = [big.tile([P, 4, 1024], BF16, name="t_tile", tag="ld", bufs=4, align_bytes=64) for g in range(2)]
+        r_in = [keep.tile([P, 4, 1024], BF16, name="r_tile%d" % g, align_bytes=64) for g in range(2)]
+        u_in = [keep.tile([P, 4, 1024], BF16, name="u_tile%d" % g, align_bytes=64) for g in range(2)]
+        t_rows = t.rearrange("(i p) d -> p i d", p=P)
+        for item in LOADS.split():
+            g = int(item[1])
+            if item[0] == "t":
+                nc.sync.dma_start(out=t_in[g // 2][:, 2 * (g % 2) : 2 * (g % 2) + 2, :], in_=t_rows[:, 2 * g : 2 * g + 2, :])
+            elif item[0] == "r":
+                rows = r[512 * (g // 2) : 512 * (g // 2 + 1), :].rearrange("(p j) d -> p j d", j=4)
+                nc.sync.dma_start(out=r_in[g // 2][:, 2 * (g % 2) : 2 * (g % 2) + 2, :], in_=rows[:, 2 * (g % 2) : 2 * (g % 2) + 2, :])
+            else:
+                nc.sync.dma_start(out=u_in[g][:], in_=u[512 * g : 512 * (g + 1), :].rearrange("(p j) c -> p j c", j=4))
+
+        ident = keep.tile([P, P], F32, name="ident", align_bytes=64)
+        make_identity(nc, ident[:])
+        warm = keep.tile([P, 1], F32, name="warm")
+        nc.scalar.activation(out=warm[:], in_=ident[:, 0:1], func=ACT.Sigmoid)
+
+        ab32 = keep.tile([P, 2, 8], F32, name="ab32")
+
+        rt_codes = keep.tile([P, 8, 2, P], U32, name="rt_codes", align_bytes=64)
+        rt_scales = keep.tile([P, 8, 2, P], U8, name="rt_scales", align_bytes=64)
+        tt_codes = keep.tile([P, 2, 2, 512], U32, name="tt_codes", align_bytes=64)
+        tt_scales = keep.tile([P, 2, 2, 512], U8, name="tt_scales", align_bytes=64)
+        rn_codes = keep.tile([P, 2, 2, 512], U32, name="rn_codes", align_bytes=64)
+        rn_scales = keep.tile([P, 2, 2, 512], U8, name="rn_scales", align_bytes=64)
+        p_scales = keep.tile([P, 2, 1024], U8, name="p_scales", align_bytes=64)
+
+        def turn(rows):
+            words = rows.bitcast(F32)
+            bank = psum.tile([P, 512], F32, name="bank", tag="bank", bufs=8)
+            view = bank[:].rearrange("p (k w n) -> p k w n", k=2, w=2)
+            for k in range(2):
+                for w in range(2):
+                    nc.tensor.transpose(view[:, k, w, :], words[:, 256 * k + w : 256 * (k + 1) : 2], ident[:])
+            return view.rearrange("p k w n -> p k n w")
+
+        def copy_same(eng, out, in_):
+            if eng == "s":
+                nc.scalar.copy(out=out, in_=in_)
+            else:
+                nc.vector.tensor_copy(out=out, in_=in_)
+
+        gt = {}
+        gr = {}
+        rn_in = {}
+        w_fac = {}
+        prob = {}
+        banks = {}
+        vs = {}
+        lg = {}
+        q2 = {}
+        es = {}
+        ec = {}
+        pb = {}
+        ro = {}
+
+        def Tt(h, i, e):
+            if h not in gt:
+                grouped = big.tile([P, 2, 2048], BF16, name="grouped", tag="g8", bufs=2, align_bytes=64)
+                gt[h] = grouped
+            copy_same(e, gt[h][:, :, 512 * i : 512 * (i + 1)].bitcast(F32).rearrange("p k (n w) -> p k n w", w=2), turn(t_in[h][:, i, :]))
+
+        def Qt(h, k):
+            nc.vector.quantize_mx(out=tt_codes[:, h, k, :].bitcast(FP8X4), scales=tt_scales[:, h, k, :], in_=gt[h][:, k, :])
+
+        def Tr(s, e):
+            if s // 2 not in gr:
+                grouped = work.tile([P, 2048], BF16, name="grouped_r", tag="gr", bufs=2, align_bytes=64)
+                gr[s // 2] = grouped
+            i = s % 2
+            copy_same(e, gr[s // 2][:, 1024 * i : 1024 * (i + 1)].bitcast(F32).rearrange("p (k n w) -> p k n w", k=2, w=2), turn(r_in[s // 4][:, s % 4, :]))
+
+        def Qr(pair):
+            s = 2 * pair
+            nc.vector.quantize_mx(
+                out=rt_codes[:, s : s + 2, :, :].rearrange("p s k n -> p (s k n)").bitcast(FP8X4),
+                scales=rt_scales[:, s : s + 2, :, :].rearrange("p s k n -> p (s k n)"),
+                in_=gr[pair][:],
+            )
+
+        def L(g, k, e):
+            if g not in rn_in:
+                rn = big.tile([P, 2, 2048], BF16, name="rn", tag="g8", bufs=2, align_bytes=64)
+                rn_in[g] = rn
+            out = rn_in[g][:, k, :].rearrange("p (t m j) -> p t m j", t=4, j=4)
+            in_ = r_in[g][:, :, 512 * k : 512 * (k + 1)].rearrange("p j (m t) -> p t m j", t=4)
+            if e == "g":
+                nc.gpsimd.tensor_scalar(out=out, in0=in_, scalar1=1.0, scalar2=0.0, op0=ALU.mult, op1=ALU.add)
+            else:
+                copy_same(e, out, in_)
+
+        def Qn(g, k):
+            nc.vector.quantize_mx(out=rn_codes[:, g, k, :].bitcast(FP8X4), scales=rn_scales[:, g, k, :], in_=rn_in[g][:, k, :])
+
+        def AB():
+            nc.vector.tensor_scalar(out=ab32[:, 0, :], in0=a_in[:], scalar1=2.0, scalar2=None, op0=ALU.mult)
+            nc.vector.tensor_copy(out=ab32[:, 1, :], in_=b_in[:])
+
+        def S(g, e):
+            eng = nc.vector if e == "v" else nc.gpsimd
+            eng.tensor_scalar(out=u_in[g][:], in0=u_in[g][:], scalar1=0.7, scalar2=0.5, op0=ALU.is_gt, op1=ALU.subtract)
+
+        def W(g, h, e):
+            wt = big.tile([P, 4, 512], F32, name="wt", tag="ld", bufs=4, align_bytes=64)
+            w_fac[g, h] = wt
+            eng = nc.vector if e == "v" else nc.gpsimd
+            for j in range(4):
+                eng.tensor_scalar(
+                    out=wt[:, j, :], in0=u_in[g][:, j, 512 * h : 512 * (h + 1)],
+                    scalar1=0.25, scalar2=ab32[:, 0, 4 * g + j : 4 * g + j + 1], op0=ALU.subtract, op1=ALU.mult,
+                )
+
+        def M(g, h):
+            for j in range(4):
+                bank = psum.tile([P, 512], F32, name="bank", tag="bank", bufs=8)
+                for k in range(2):
+                    nc.tensor.matmul_mx(
+                        out=bank[:],
+                        lhsT=rt_codes[:, 4 * g + j, k, :].bitcast(FP8X4), lhsT_scale=rt_scales[:, 4 * g + j, k, :],
+                        rhs=tt_codes[:, h, k, :].bitcast(FP8X4), rhs_scale=tt_scales[:, h, k, :],
+                        start=(k == 0), stop=(k == 1),
+                    )
+                banks[g, h, j] = bank
+
+        def V(g, h, j):
+            s = 4 * g + j
+            v = work.tile([P, 512], F32, name="v", tag="v", bufs=6, align_bytes=64)
+            nc.vector.scalar_tensor_tensor(
+                out=v[:], in0=banks[g, h, j][:], scalar=ab32[:, 1, s : s + 1],
+                in1=u_in[g][:, j, 512 * h : 512 * (h + 1)], op0=ALU.add, op1=ALU.mult,
+            )
+            vs[g, h, j] = v
+
+        def A(g, h, j):
+            if (g, h) not in prob:
+                pt = keep.tile([P, 4, 512], F32, name="prob%d%d" % (g, h), align_bytes=64)
+                prob[g, h] = pt
+            s = 4 * g + j
+            nc.scalar.activation(out=prob[g, h][:, j, :], in_=vs[g, h, j][:], func=ACT.Sigmoid, scale=ab32[:, 0, s : s + 1])
+
+        def where(i):
+            c0, w = BLOCKS[i]
+            return c0 // 512, c0 % 512, w
+
+        def Ln(i, g):
+            h, o, w = where(i)
+            l = work.tile([P, 4, w], F32, name="l", tag="l", bufs=4, align_bytes=64)
+            nc.scalar.activation(out=l[:], in_=prob[g, h][:, :, o : o + w], func=ACT.Ln, bias=2.0 ** -64)
+            lg[i, g] = l
+
+        def Sq(i, g):
+            h, o, w = where(i)
+            q = work.tile([P, 4, w], F32, name="q", tag="q", bufs=3, align_bytes=64)
+            nc.scalar.activation(out=q[:], in_=prob[g, h][:, :, o : o + w], func=ACT.Square, scale=-1.0, bias=1.0)
+            q2[i, g] = q
+
+        def B(i, g):
+            h, o, w = where(i)
+            l = lg[i, g]
+            nc.vector.scalar_tensor_tensor(out=l[:], in0=l[:], scalar=0.5, in1=prob[g, h][:, :, o : o + w], op0=ALU.add, op1=ALU.mult)
+
+        def X(i, g):
+            h, o, w = where(i)
+            l = lg[i, g]
+            nc.vector.scalar_tensor_tensor(out=l[:], in0=l[:], scalar=0.5, in1=w_fac[g, h][:, :, o : o + w], op0=ALU.subtract, op1=ALU.mult)
+
+        def E(i, g):
+            h, o, w = where(i)
+            e = work.tile([P, w, 4], BF16, name="e", tag="e", bufs=3, align_bytes=64)
+            nc.vector.tensor_tensor(
+                out=e[:].rearrange("p (c i) t -> p c t i", i=4),
+                in0=lg[i, g][:].rearrange("p t (c i) -> p c t i", i=4),
+                in1=q2[i, g][:].rearrange("p t (c i) -> p c t i", i=4), op=ALU.mult,
+            )
+            es[i, g] = e
+
+        def Qe(i, g):
+            h, o, w = where(i)
+            codes = work.tile([P, w], U32, name="e_codes", tag="ec", bufs=4, align_bytes=64)
+            scales = work.tile([P, w], U8, name="e_scales", tag="es", bufs=4, align_bytes=64)
+            nc.vector.quantize_mx(out=codes[:].bitcast(FP8X4), scales=scales[:], in_=es[i, g][:].rearrange("p c t -> p (c t)"))
+            ec[i, g] = (codes, scales)
+
+        def MP(i, ct, k):
+            cs = slice(P * ct, P * (ct + 1))
+            bank = psum.tile([P, 512], F32, name="bank", tag="bank", bufs=8)
+            for j in range(4):
+                for g in range(2):
+                    nc.tensor.matmul_mx(
+                        out=bank[:, P * j : P * (j + 1)],
+                        lhsT=rn_codes[:, g, k, P * j : P * (j + 1)].bitcast(FP8X4), lhsT_scale=rn_scales[:, g, k, P * j : P * (j + 1)],
+                        rhs=ec[i, g][0][:, cs].bitcast(FP8X4), rhs_scale=ec[i, g][1][:, cs],
+                        start=(g == 0), stop=(g == 1),
+                    )
+            banks["p", i, ct, k] = bank
+
+        def MR(i, ct, k):
+            cs = slice(P * ct, P * (ct + 1))
+            bank = psum.tile([P, 512], F32, name="bank", tag="bank", bufs=8)
+            for g in range(2):
+                nc.tensor.matmul_mx(
+                    out=bank[:],
+                    lhsT=ec[i, g][0][:, cs].bitcast(FP8X4), lhsT_scale=ec[i, g][1][:, cs],
+                    rhs=rn_codes[:, g, k, :].bitcast(FP8X4), rhs_scale=rn_scales[:, g, k, :],
+                    start=(g == 0), stop=(g == 1),
+                )
+            banks["r", i, ct, k] = bank
+
+        def copy_eighth(eng, out, in_):
+            if eng == "s":
+                nc.scalar.mul(out=out, in_=in_, mul=0.125)
+            else:
+                nc.vector.tensor_scalar(out=out, in0=in_, scalar1=0.125, scalar2=None, op0=ALU.mult)
+
+        def OP(i, ct, k, e):
+            h, o, w = where(i)
+            if (i, k) not in pb:
+                pbt = work.tile([P, w * 4], BF16, name="pbt", tag="pb", bufs=4, align_bytes=64)
+                pb[i, k] = pbt
+            copy_eighth(
+                e, pb[i, k][:, 512 * ct : 512 * (ct + 1)].rearrange("p (c t) -> p c t", t=4),
+                banks["p", i, ct, k][:].rearrange("p (t c) -> p c t", t=4),
+            )
+
+        def OR(i, ct, k, e):
+            c0 = BLOCKS[i][0]
+            if (i, ct) not in ro:
+                rot = work.tile([P, 1024], F32, name="rot", tag="ro", bufs=3, align_bytes=64)
+                ro[i, ct] = rot
+            copy_eighth(
+                e, ro[i, ct][:, 512 * k : 512 * (k + 1)].rearrange("p (m t) -> p m t", t=4),
+                banks["r", i, ct, k][:].rearrange("p (t m) -> p m t", t=4),
+            )
+            if k == 1:
+                nc.sync.dma_start(out=out_0[c0 + P * ct : c0 + P * (ct + 1), :], in_=ro[i, ct][:])
+
+        def QP(i, k):
+            c0, w = BLOCKS[i]
+            pc = work.tile([P, w], U32, name="pc", tag="pc", bufs=4, align_bytes=64)
+            nc.vector.quantize_mx(out=pc[:].bitcast(FP8X4), scales=p_scales[:, k, c0 : c0 + w], in_=pb[i, k][:])
+            nc.sync.dma_start(out=out_1[k, :, c0 : c0 + w, :].rearrange("p m t -> p (m t)").bitcast(I32), in_=pc[:].bitcast(I32))
+
+        def SC(c0, c1):
+            for q in range(4):
+                nc.sync.dma_start(
+                    out=out_2[:, 4 * q : 4 * q + 4, c0:c1].bitcast(I32).rearrange("k r c -> r k c"),
+                    in_=p_scales[32 * q : 32 * q + 4, :, c0:c1].bitcast(I32),
+                )
+
+        steps = {
+            "Tt": Tt, "Qt": Qt, "Tr": Tr, "Qr": Qr, "L": L, "Qn": Qn, "AB": AB, "S": S, "W": W, "M": M, "V": V, "A": A,
+            "Ln": Ln, "Sq": Sq, "B": B, "X": X, "E": E, "Qe": Qe, "MP": MP, "MR": MR, "OP": OP, "OR": OR, "QP": QP, "SC": SC,
+        }
+
+        def run(text):
+            for item in text.split():
+                parts = item.split(",")
+                steps[parts[0]](*[x if x in "svg" else int(x) for x in parts[1:]])
+
+        run(HEAD)
+        run(TAIL)

@@ -17,9 +17,9 @@ ACT = mybir.ActivationFunctionType
 
 P = 128
 BLOCKS = [(0, 256), (256, 256), (512, 256), (768, 128), (896, 128)]
-LOADS = "t0 t1 r0 r1 u0 t2 t3 r2 r3 u1"
-HEAD = "AB Tt,0,0,s Tt,0,1,v Tt,0,2,s Tt,0,3,v Tr,0,s Tr,1,v Tr,2,s Tr,3,s Qt,0,0 Qt,0,1 Qr,0 L,0,0,s L,0,1,s Qr,1 M,0,0 S,0,v V,0,0,0 V,0,0,1 V,0,0,2 V,0,0,3 Tt,1,0,s Tt,1,1,s Tt,1,2,s Tt,1,3,s Qn,0,0 Qn,0,1 W,0,0,g Qt,1,0 Qt,1,1 Tr,4,s Tr,5,s Tr,6,s Tr,7,s A,0,0,0 A,0,0,1 A,0,0,2 A,0,0,3 M,0,1 W,0,1,v V,0,1,0 V,0,1,1 S,1,v Qr,2 V,0,1,2 Qr,3 V,0,1,3 M,1,0 A,0,1,0 A,0,1,1 A,0,1,2 A,0,1,3 W,1,0,g W,1,1,g V,1,0,0 V,1,0,1 V,1,0,2 V,1,0,3 A,1,0,0 A,1,0,1 A,1,0,2 A,1,0,3 M,1,1 V,1,1,0 V,1,1,1 V,1,1,2 V,1,1,3 A,1,1,0 A,1,1,1 A,1,1,2 A,1,1,3 L,1,0,v L,1,1,v Qn,1,0 Qn,1,1"
-TAIL = "Ln,0,0 Ln,0,1 Sq,0,0 Sq,0,1 B,0,0 B,0,1 X,0,0 X,0,1 E,0,0 E,0,1 Qe,0,0 Qe,0,1 MP,0,0,0 MP,0,0,1 MR,0,0,0 MR,0,0,1 MP,0,1,0 MP,0,1,1 MR,0,1,0 MR,0,1,1 Ln,1,0 Ln,1,1 Sq,1,0 Sq,1,1 B,1,0 B,1,1 X,1,0 X,1,1 E,1,0 E,1,1 Qe,1,0 Qe,1,1 OP,0,0,0,s OP,0,0,1,s OR,0,0,0,s OR,0,0,1,v OP,0,1,0,s OP,0,1,1,s OR,0,1,0,s OR,0,1,1,s QP,0,0 QP,0,1 MP,1,0,0 MP,1,0,1 MR,1,0,0 MR,1,0,1 MP,1,1,0 MP,1,1,1 MR,1,1,0 MR,1,1,1 Ln,2,0 Ln,2,1 Sq,2,0 Sq,2,1 B,2,0 B,2,1 X,2,0 X,2,1 E,2,0 E,2,1 Qe,2,0 Qe,2,1 OP,1,0,0,s OP,1,0,1,s OR,1,0,0,s OR,1,0,1,v OP,1,1,0,s OP,1,1,1,s OR,1,1,0,s OR,1,1,1,s QP,1,0 QP,1,1 MP,2,0,0 MP,2,0,1 MR,2,0,0 MR,2,0,1 MP,2,1,0 MP,2,1,1 MR,2,1,0 MR,2,1,1 Ln,3,0 Ln,3,1 Sq,3,0 Sq,3,1 B,3,0 B,3,1 X,3,0 X,3,1 E,3,0 E,3,1 Qe,3,0 Qe,3,1 OP,2,0,0,s OP,2,0,1,s OR,2,0,0,s OR,2,0,1,v OP,2,1,0,s OP,2,1,1,s OR,2,1,0,s OR,2,1,1,s QP,2,0 QP,2,1 MP,3,0,0 MP,3,0,1 MR,3,0,0 MR,3,0,1 Ln,4,0 Ln,4,1 Sq,4,0 Sq,4,1 B,4,0 B,4,1 X,4,0 X,4,1 E,4,0 E,4,1 Qe,4,0 Qe,4,1 OP,3,0,0,s OP,3,0,1,s OR,3,0,0,s OR,3,0,1,v QP,3,0 QP,3,1 MP,4,0,0 MP,4,0,1 MR,4,0,0 MR,4,0,1 SC,0,896 OP,4,0,0,s OP,4,0,1,s OR,4,0,0,s OR,4,0,1,v QP,4,0 QP,4,1 SC,896,1024"
+LOADS = "t01 t11 t22 r0 r1 u0 t42 t62 r2 r3 u1"
+HEAD = "AB D,6 Tt,0,0,s Tt,0,1,v D,1 D,1 Tt,0,2,s Tt,0,3,v D,1 Qt,0,0 D,1 L,0,0,s D,1 Tr,2,s Qt,0,1 Tr,1,v Tr,0,s D,1 Qr,0 D,1 Tr,3,s S,0,v Tt,1,0,s M,0,0,1 M,0,0,0 Qr,1 L,0,1,s W,0,0,v M,0,0,3 V,0,0,1 M,0,0,2 Tt,1,2,s Tt,1,1,s Tt,1,3,s V,0,0,0 V,0,0,2 V,0,0,3 Qn,0,0 Tr,4,s Tr,7,s Tr,5,s Qt,1,0 Qt,1,1 A,0,0,2 D,1 M,0,1,0 M,0,1,1 M,0,1,2 A,0,0,1 W,0,1,v A,0,0,0 V,0,1,0 A,0,1,0 Tr,6,s V,0,1,1 M,0,1,3 A,0,1,1 V,0,1,2 Qn,0,1 V,0,1,3 Qr,2 S,1,v M,1,0,0 Qr,3 M,1,0,1 V,1,0,0 A,0,0,3 A,0,1,2 V,1,0,1 M,1,0,2 M,1,1,0 A,0,1,3 M,1,1,2 A,1,0,0 M,1,0,3 V,1,0,2 A,1,0,1 V,1,1,0 D,1 W,1,1,v A,1,0,2 M,1,1,1 V,1,0,3 A,1,1,0 M,1,1,3 A,1,0,3 V,1,1,1 V,1,1,2 A,1,1,1 V,1,1,3 W,1,0,v L,1,0,v A,1,1,2 L,1,1,v A,1,1,3 Qn,1,0 Qn,1,1"
+TAIL = "Ln,0,0 Ln,0,1 Sq,0,0 Sq,0,1 B,0,0 B,0,1 X,0,0 X,0,1 E,0,0 E,0,1 Qe,0,0 Qe,0,1 MP,0,0,0 MP,0,0,1 MR,0,0,0 MR,0,0,1 MP,0,1,0 MP,0,1,1 MR,0,1,0 MR,0,1,1 Ln,1,0 Ln,1,1 Sq,1,0 Sq,1,1 B,1,0 B,1,1 X,1,0 X,1,1 E,1,0 E,1,1 Qe,1,0 Qe,1,1 OP,0,0,0,s OP,0,0,1,s OR,0,0,0,s OR,0,0,1,s OP,0,1,0,s OP,0,1,1,s OR,0,1,0,s OR,0,1,1,s QP,0,0 QP,0,1 MP,1,0,0 MP,1,0,1 MR,1,0,0 MR,1,0,1 MP,1,1,0 MP,1,1,1 MR,1,1,0 MR,1,1,1 Ln,2,0 Ln,2,1 Sq,2,0 Sq,2,1 B,2,0 B,2,1 X,2,0 X,2,1 E,2,0 E,2,1 Qe,2,0 Qe,2,1 OP,1,0,0,s OP,1,0,1,s OR,1,0,0,s OR,1,0,1,s OP,1,1,0,s OP,1,1,1,s OR,1,1,0,s OR,1,1,1,s QP,1,0 QP,1,1 MP,2,0,0 MP,2,0,1 MR,2,0,0 MR,2,0,1 MP,2,1,0 MP,2,1,1 MR,2,1,0 MR,2,1,1 Ln,3,0 Ln,3,1 Sq,3,0 Sq,3,1 B,3,0 B,3,1 X,3,0 X,3,1 E,3,0 E,3,1 Qe,3,0 Qe,3,1 OP,2,0,0,s OP,2,0,1,s OR,2,0,0,s OR,2,0,1,s OP,2,1,0,s OP,2,1,1,s OR,2,1,0,s OR,2,1,1,s QP,2,0 QP,2,1 MP,3,0,0 MP,3,0,1 MR,3,0,0 MR,3,0,1 Ln,4,0 Ln,4,1 Sq,4,0 Sq,4,1 B,4,0 B,4,1 X,4,0 X,4,1 E,4,0 E,4,1 Qe,4,0 Qe,4,1 OP,3,0,0,s OP,3,0,1,s OR,3,0,0,s OR,3,0,1,s QP,3,0 QP,3,1 MP,4,0,0 MP,4,0,1 MR,4,0,0 MR,4,0,1 SC,0,896 OP,4,0,0,s OP,4,0,1,v OR,4,0,0,s OR,4,0,1,v QP,4,0 QP,4,1 SC,896,1024"
 
 
 def tile_owlshiftscalefocaltextgradient_x1_kernel(tc, r, t, a, b, u, out_0, out_1, out_2):
@@ -42,7 +42,8 @@ def tile_owlshiftscalefocaltextgradient_x1_kernel(tc, r, t, a, b, u, out_0, out_
         for item in LOADS.split():
             g = int(item[1])
             if item[0] == "t":
-                nc.sync.dma_start(out=t_in[g // 2][:, 2 * (g % 2) : 2 * (g % 2) + 2, :], in_=t_rows[:, 2 * g : 2 * g + 2, :])
+                n = int(item[2])
+                nc.sync.dma_start(out=t_in[g // 4][:, g % 4 : g % 4 + n, :], in_=t_rows[:, g : g + n, :])
             elif item[0] == "r":
                 rows = r[512 * (g // 2) : 512 * (g // 2 + 1), :].rearrange("(p j) d -> p j d", j=4)
                 nc.sync.dma_start(out=r_in[g // 2][:, 2 * (g % 2) : 2 * (g % 2) + 2, :], in_=rows[:, 2 * (g % 2) : 2 * (g % 2) + 2, :])
@@ -53,6 +54,14 @@ def tile_owlshiftscalefocaltextgradient_x1_kernel(tc, r, t, a, b, u, out_0, out_
         make_identity(nc, ident[:])
         warm = keep.tile([P, 1], F32, name="warm")
         nc.scalar.activation(out=warm[:], in_=ident[:, 0:1], func=ACT.Sigmoid)
+
+        zeros = keep.tile([P, 512], BF16, name="zeros", align_bytes=64)
+        nc.vector.memset(zeros[:], 0.0)
+
+        def D(n):
+            bank = psum.tile([P, 512], F32, name="bank", tag="bank", bufs=8)
+            for i in range(n):
+                nc.tensor.matmul(bank[:], lhsT=zeros[:, 0:P], rhs=zeros[:], start=True, stop=True)
 
         ab32 = keep.tile([P, 2, 8], F32, name="ab32")
 
@@ -149,17 +158,16 @@ def tile_owlshiftscalefocaltextgradient_x1_kernel(tc, r, t, a, b, u, out_0, out_
                     scalar1=0.25, scalar2=ab32[:, 0, 4 * g + j : 4 * g + j + 1], op0=ALU.subtract, op1=ALU.mult,
                 )
 
-        def M(g, h):
-            for j in range(4):
-                bank = psum.tile([P, 512], F32, name="bank", tag="bank", bufs=8)
-                for k in range(2):
-                    nc.tensor.matmul_mx(
-                        out=bank[:],
-                        lhsT=rt_codes[:, 4 * g + j, k, :].bitcast(FP8X4), lhsT_scale=rt_scales[:, 4 * g + j, k, :],
-                        rhs=tt_codes[:, h, k, :].bitcast(FP8X4), rhs_scale=tt_scales[:, h, k, :],
-                        start=(k == 0), stop=(k == 1),
-                    )
-                banks[g, h, j] = bank
+        def M(g, h, j):
+            bank = psum.tile([P, 512], F32, name="bank", tag="bank", bufs=8)
+            for k in range(2):
+                nc.tensor.matmul_mx(
+                    out=bank[:],
+                    lhsT=rt_codes[:, 4 * g + j, k, :].bitcast(FP8X4), lhsT_scale=rt_scales[:, 4 * g + j, k, :],
+                    rhs=tt_codes[:, h, k, :].bitcast(FP8X4), rhs_scale=tt_scales[:, h, k, :],
+                    start=(k == 0), stop=(k == 1),
+                )
+            banks[g, h, j] = bank
 
         def V(g, h, j):
             s = 4 * g + j
@@ -207,9 +215,9 @@ def tile_owlshiftscalefocaltextgradient_x1_kernel(tc, r, t, a, b, u, out_0, out_
             h, o, w = where(i)
             e = work.tile([P, w, 4], BF16, name="e", tag="e", bufs=3, align_bytes=64)
             nc.vector.tensor_tensor(
-                out=e[:].rearrange("p (c i) t -> p c t i", i=4),
-                in0=lg[i, g][:].rearrange("p t (c i) -> p c t i", i=4),
-                in1=q2[i, g][:].rearrange("p t (c i) -> p c t i", i=4), op=ALU.mult,
+                out=e[:].rearrange("p (c i) t -> p c t i", i=2),
+                in0=lg[i, g][:].rearrange("p t (c i) -> p c t i", i=2),
+                in1=q2[i, g][:].rearrange("p t (c i) -> p c t i", i=2), op=ALU.mult,
             )
             es[i, g] = e
 
@@ -287,6 +295,7 @@ def tile_owlshiftscalefocaltextgradient_x1_kernel(tc, r, t, a, b, u, out_0, out_
                 )
 
         steps = {
+            "D": D,
             "Tt": Tt, "Qt": Qt, "Tr": Tr, "Qr": Qr, "L": L, "Qn": Qn, "AB": AB, "S": S, "W": W, "M": M, "V": V, "A": A,
             "Ln": Ln, "Sq": Sq, "B": B, "X": X, "E": E, "Qe": Qe, "MP": MP, "MR": MR, "OP": OP, "OR": OR, "QP": QP, "SC": SC,
         }

@@ -4,7 +4,7 @@ import concourse.mybir as mybir
 from concourse.masks import make_identity
 
 N, D, C = 1024, 1024, 1024
-FLOPS = 2 * N * D * C * 2
+FLOPS = 2 * (2 * N * D * C)
 
 F32 = mybir.dt.float32
 BF16 = mybir.dt.bfloat16
@@ -16,294 +16,400 @@ ALU = mybir.AluOpType
 ACT = mybir.ActivationFunctionType
 
 P = 128
-BLOCKS = [(0, 256), (256, 256), (512, 256), (768, 128), (896, 128)]
-LOADS = "t01 t11 t22 r0 r1 u0 t42 t62 r2 r3 u1"
-HEAD = "AB D,6 Tt,0,0,s Tt,0,1,v D,1 D,1 Tt,0,2,s Tt,0,3,v D,1 Qt,0,0 D,1 L,0,0,s D,1 Tr,2,s Qt,0,1 Tr,1,v Tr,0,s D,1 Qr,0 D,1 Tr,3,s S,0,v Tt,1,0,s M,0,0,1 M,0,0,0 Qr,1 L,0,1,s W,0,0,v M,0,0,3 V,0,0,1 M,0,0,2 Tt,1,2,s Tt,1,1,s Tt,1,3,s V,0,0,0 V,0,0,2 V,0,0,3 Qn,0,0 Tr,4,s Tr,7,s Tr,5,s Qt,1,0 Qt,1,1 A,0,0,2 D,1 M,0,1,0 M,0,1,1 M,0,1,2 A,0,0,1 W,0,1,v A,0,0,0 V,0,1,0 A,0,1,0 Tr,6,s V,0,1,1 M,0,1,3 A,0,1,1 V,0,1,2 Qn,0,1 V,0,1,3 Qr,2 S,1,v M,1,0,0 Qr,3 M,1,0,1 V,1,0,0 A,0,0,3 A,0,1,2 V,1,0,1 M,1,0,2 M,1,1,0 A,0,1,3 M,1,1,2 A,1,0,0 M,1,0,3 V,1,0,2 A,1,0,1 V,1,1,0 D,1 W,1,1,v A,1,0,2 M,1,1,1 V,1,0,3 A,1,1,0 M,1,1,3 A,1,0,3 V,1,1,1 V,1,1,2 A,1,1,1 V,1,1,3 W,1,0,v L,1,0,v A,1,1,2 L,1,1,v A,1,1,3 Qn,1,0 Qn,1,1"
-TAIL = "Ln,0,0 Ln,0,1 Sq,0,0 Sq,0,1 B,0,0 B,0,1 X,0,0 X,0,1 E,0,0 E,0,1 Qe,0,0 Qe,0,1 MP,0,0,0 MP,0,0,1 MR,0,0,0 MR,0,0,1 MP,0,1,0 MP,0,1,1 MR,0,1,0 MR,0,1,1 Ln,1,0 Ln,1,1 Sq,1,0 Sq,1,1 B,1,0 B,1,1 X,1,0 X,1,1 E,1,0 E,1,1 Qe,1,0 Qe,1,1 OP,0,0,0,s OP,0,0,1,s OR,0,0,0,s OR,0,0,1,s OP,0,1,0,s OP,0,1,1,s OR,0,1,0,s OR,0,1,1,s QP,0,0 QP,0,1 MP,1,0,0 MP,1,0,1 MR,1,0,0 MR,1,0,1 MP,1,1,0 MP,1,1,1 MR,1,1,0 MR,1,1,1 Ln,2,0 Ln,2,1 Sq,2,0 Sq,2,1 B,2,0 B,2,1 X,2,0 X,2,1 E,2,0 E,2,1 Qe,2,0 Qe,2,1 OP,1,0,0,s OP,1,0,1,s OR,1,0,0,s OR,1,0,1,s OP,1,1,0,s OP,1,1,1,s OR,1,1,0,s OR,1,1,1,s QP,1,0 QP,1,1 MP,2,0,0 MP,2,0,1 MR,2,0,0 MR,2,0,1 MP,2,1,0 MP,2,1,1 MR,2,1,0 MR,2,1,1 Ln,3,0 Ln,3,1 Sq,3,0 Sq,3,1 B,3,0 B,3,1 X,3,0 X,3,1 E,3,0 E,3,1 Qe,3,0 Qe,3,1 OP,2,0,0,s OP,2,0,1,s OR,2,0,0,s OR,2,0,1,s OP,2,1,0,s OP,2,1,1,s OR,2,1,0,s OR,2,1,1,s QP,2,0 QP,2,1 MP,3,0,0 MP,3,0,1 MR,3,0,0 MR,3,0,1 Ln,4,0 Ln,4,1 Sq,4,0 Sq,4,1 B,4,0 B,4,1 X,4,0 X,4,1 E,4,0 E,4,1 Qe,4,0 Qe,4,1 OP,3,0,0,s OP,3,0,1,s OR,3,0,0,s OR,3,0,1,s QP,3,0 QP,3,1 MP,4,0,0 MP,4,0,1 MR,4,0,0 MR,4,0,1 SC,0,896 OP,4,0,0,s OP,4,0,1,v OR,4,0,0,s OR,4,0,1,v QP,4,0 QP,4,1 SC,896,1024"
+BANK = 512
+HALF = 512
+THRESHOLD = 0.7
+
+BLOCKS = ((0, 256), (256, 256), (512, 256), (768, 128), (896, 128))
 
 
 def tile_owlshiftscalefocaltextgradient_x1_kernel(tc, r, t, a, b, u, out_0, out_1, out_2):
     nc = tc.nc
     with ExitStack() as ctx:
         keep = ctx.enter_context(tc.tile_pool(name="keep", bufs=1))
-        big = ctx.enter_context(tc.tile_pool(name="big", bufs=4))
         work = ctx.enter_context(tc.tile_pool(name="work", bufs=4))
         psum = ctx.enter_context(tc.psum_pool(name="psum", bufs=8))
         ctx.enter_context(tc.manual_schedule())
 
         a_in = keep.tile([P, 8], BF16, name="a_in", align_bytes=64)
         b_in = keep.tile([P, 8], BF16, name="b_in", align_bytes=64)
-        nc.scalar.dma_start(out=a_in[:].rearrange("p (g t) -> p g t", t=4), in_=a.rearrange("(g p t) -> p g t", p=P, t=4))
-        nc.scalar.dma_start(out=b_in[:].rearrange("p (g t) -> p g t", t=4), in_=b.rearrange("(g p t) -> p g t", p=P, t=4))
-        t_in = [big.tile([P, 4, 1024], BF16, name="t_tile", tag="ld", bufs=4, align_bytes=64) for g in range(2)]
-        r_in = [keep.tile([P, 4, 1024], BF16, name="r_tile%d" % g, align_bytes=64) for g in range(2)]
-        u_in = [keep.tile([P, 4, 1024], BF16, name="u_tile%d" % g, align_bytes=64) for g in range(2)]
-        t_rows = t.rearrange("(i p) d -> p i d", p=P)
-        for item in LOADS.split():
-            g = int(item[1])
-            if item[0] == "t":
-                n = int(item[2])
-                nc.sync.dma_start(out=t_in[g // 4][:, g % 4 : g % 4 + n, :], in_=t_rows[:, g : g + n, :])
-            elif item[0] == "r":
-                rows = r[512 * (g // 2) : 512 * (g // 2 + 1), :].rearrange("(p j) d -> p j d", j=4)
-                nc.sync.dma_start(out=r_in[g // 2][:, 2 * (g % 2) : 2 * (g % 2) + 2, :], in_=rows[:, 2 * (g % 2) : 2 * (g % 2) + 2, :])
-            else:
-                nc.sync.dma_start(out=u_in[g][:], in_=u[512 * g : 512 * (g + 1), :].rearrange("(p j) c -> p j c", j=4))
+        for vec, dst in ((a, a_in), (b, b_in)):
+            nc.scalar.dma_start(out=dst[:].rearrange("p (g j) -> p g j", j=4), in_=vec.rearrange("(g p j) -> p g j", p=P, j=4))
+
+        t_in = [work.tile([P, 4, D], BF16, name="t_in", tag="t_or_weight", bufs=4, align_bytes=64) for h in range(2)]
+        r_in = [keep.tile([P, 4, D], BF16, name="r_in%d" % g, align_bytes=64) for g in range(2)]
+        u_in = [keep.tile([P, 4, C], BF16, name="u_in%d" % g, align_bytes=64) for g in range(2)]
+
+        def load_t(h, i, n):
+            rows = t[HALF * h : HALF * (h + 1), :].rearrange("(i p) d -> p i d", p=P)
+            nc.sync.dma_start(out=t_in[h][:, i : i + n, :], in_=rows[:, i : i + n, :])
+
+        def load_regions(dst, src, g, j, n):
+            rows = src[512 * g : 512 * (g + 1), :].rearrange("(p j) c -> p j c", j=4)
+            nc.sync.dma_start(out=dst[g][:, j : j + n, :], in_=rows[:, j : j + n, :])
+
+        load_t(0, 0, 2)
+        load_regions(u_in, u, 0, 0, 2)
+        load_t(0, 2, 1)
+        load_t(0, 3, 1)
+        load_regions(u_in, u, 0, 2, 2)
+        load_regions(r_in, r, 0, 0, 2)
+        load_regions(r_in, r, 0, 2, 2)
+        load_t(1, 0, 2)
+        load_t(1, 2, 2)
+        load_regions(r_in, r, 1, 0, 2)
+        load_regions(r_in, r, 1, 2, 2)
+        load_regions(u_in, u, 1, 0, 4)
 
         ident = keep.tile([P, P], F32, name="ident", align_bytes=64)
         make_identity(nc, ident[:])
-        warm = keep.tile([P, 1], F32, name="warm")
-        nc.scalar.activation(out=warm[:], in_=ident[:, 0:1], func=ACT.Sigmoid)
-
-        zeros = keep.tile([P, 512], BF16, name="zeros", align_bytes=64)
+        table_warm_up = keep.tile([P, 1], F32, name="table_warm_up")
+        nc.scalar.activation(out=table_warm_up[:], in_=ident[:, 0:1], func=ACT.Sigmoid)
+        zeros = keep.tile([P, BANK], BF16, name="zeros", align_bytes=64)
         nc.vector.memset(zeros[:], 0.0)
 
-        def D(n):
-            bank = psum.tile([P, 512], F32, name="bank", tag="bank", bufs=8)
+        a2 = keep.tile([P, 8], F32, name="a2", align_bytes=64)
+        b1 = keep.tile([P, 8], F32, name="b1", align_bytes=64)
+        ah = keep.tile([P, 8], F32, name="ah", align_bytes=64)
+
+        rd_codes = keep.tile([P, 8, 2, P], U32, name="rd_codes", align_bytes=64)
+        rd_scales = keep.tile([P, 8, 2, P], U8, name="rd_scales", align_bytes=64)
+        td_codes = keep.tile([P, 2, 2, HALF], U32, name="td_codes", align_bytes=64)
+        td_scales = keep.tile([P, 2, 2, HALF], U8, name="td_scales", align_bytes=64)
+        rn_codes = keep.tile([P, 2, 2, 512], U32, name="rn_codes", align_bytes=64)
+        rn_scales = keep.tile([P, 2, 2, 512], U8, name="rn_scales", align_bytes=64)
+        out_scales = keep.tile([P, 2, C], U8, name="out_scales", align_bytes=64)
+
+        td_in = {}
+        rd_in = {}
+        rn_in = {}
+        weight = {}
+        prob = {}
+        bank_of = {}
+        signed = {}
+        log_of = {}
+        square_of = {}
+        e_of = {}
+        e_codes = {}
+        plane_in = {}
+        rows_out = {}
+
+        def new_bank():
+            bank = psum.tile([P, BANK], F32, name="bank", tag="bank", bufs=8)
+            return bank
+
+        def warm_up(bank, n):
             for i in range(n):
                 nc.tensor.matmul(bank[:], lhsT=zeros[:, 0:P], rhs=zeros[:], start=True, stop=True)
 
-        ab32 = keep.tile([P, 2, 8], F32, name="ab32")
-
-        rt_codes = keep.tile([P, 8, 2, P], U32, name="rt_codes", align_bytes=64)
-        rt_scales = keep.tile([P, 8, 2, P], U8, name="rt_scales", align_bytes=64)
-        tt_codes = keep.tile([P, 2, 2, 512], U32, name="tt_codes", align_bytes=64)
-        tt_scales = keep.tile([P, 2, 2, 512], U8, name="tt_scales", align_bytes=64)
-        rn_codes = keep.tile([P, 2, 2, 512], U32, name="rn_codes", align_bytes=64)
-        rn_scales = keep.tile([P, 2, 2, 512], U8, name="rn_scales", align_bytes=64)
-        p_scales = keep.tile([P, 2, 1024], U8, name="p_scales", align_bytes=64)
-
-        def turn(rows):
+        def turn(rows, copy, out, dummies):
             words = rows.bitcast(F32)
-            bank = psum.tile([P, 512], F32, name="bank", tag="bank", bufs=8)
-            view = bank[:].rearrange("p (k w n) -> p k w n", k=2, w=2)
+            bank = new_bank()
+            warm_up(bank, dummies)
+            turned = bank[:].rearrange("p (k w n) -> p k w n", k=2, w=2)
             for k in range(2):
                 for w in range(2):
-                    nc.tensor.transpose(view[:, k, w, :], words[:, 256 * k + w : 256 * (k + 1) : 2], ident[:])
-            return view.rearrange("p k w n -> p k n w")
+                    nc.tensor.transpose(turned[:, k, w, :], words[:, 256 * k + w : 256 * (k + 1) : 2], ident[:])
+            copy(out=out, in_=turned.rearrange("p k w n -> p k n w"))
 
-        def copy_same(eng, out, in_):
-            if eng == "s":
-                nc.scalar.copy(out=out, in_=in_)
-            else:
-                nc.vector.tensor_copy(out=out, in_=in_)
+        def turn_t(h, i, copy, dummies=0):
+            if h not in td_in:
+                grouped = work.tile([P, 2, 4 * HALF], BF16, name="grouped", tag="grouped", bufs=3, align_bytes=64)
+                td_in[h] = grouped
+            out = td_in[h][:, :, 512 * i : 512 * (i + 1)].bitcast(F32).rearrange("p k (n w) -> p k n w", w=2)
+            turn(t_in[h][:, i, :], copy, out, dummies)
 
-        gt = {}
-        gr = {}
-        rn_in = {}
-        w_fac = {}
-        prob = {}
-        banks = {}
-        vs = {}
-        lg = {}
-        q2 = {}
-        es = {}
-        ec = {}
-        pb = {}
-        ro = {}
+        def turn_r(g, j, copy, dummies=0):
+            pair = (g, j // 2)
+            if pair not in rd_in:
+                pair_in = work.tile([P, 2, 4 * 2 * P], BF16, name="pair_in", tag="pair_in", bufs=2, align_bytes=64)
+                rd_in[pair] = pair_in
+            out = rd_in[pair][:, j % 2, :].bitcast(F32).rearrange("p (k n w) -> p k n w", k=2, w=2)
+            turn(r_in[g][:, j, :], copy, out, dummies)
 
-        def Tt(h, i, e):
-            if h not in gt:
-                grouped = big.tile([P, 2, 2048], BF16, name="grouped", tag="g8", bufs=2, align_bytes=64)
-                gt[h] = grouped
-            copy_same(e, gt[h][:, :, 512 * i : 512 * (i + 1)].bitcast(F32).rearrange("p k (n w) -> p k n w", w=2), turn(t_in[h][:, i, :]))
+        def quantise_td(h, k):
+            nc.vector.quantize_mx(out=td_codes[:, h, k, :].bitcast(FP8X4), scales=td_scales[:, h, k, :], in_=td_in[h][:, k, :])
 
-        def Qt(h, k):
-            nc.vector.quantize_mx(out=tt_codes[:, h, k, :].bitcast(FP8X4), scales=tt_scales[:, h, k, :], in_=gt[h][:, k, :])
-
-        def Tr(s, e):
-            if s // 2 not in gr:
-                grouped = work.tile([P, 2048], BF16, name="grouped_r", tag="gr", bufs=2, align_bytes=64)
-                gr[s // 2] = grouped
-            i = s % 2
-            copy_same(e, gr[s // 2][:, 1024 * i : 1024 * (i + 1)].bitcast(F32).rearrange("p (k n w) -> p k n w", k=2, w=2), turn(r_in[s // 4][:, s % 4, :]))
-
-        def Qr(pair):
-            s = 2 * pair
+        def quantise_rd(g, half):
+            tiles = slice(4 * g + 2 * half, 4 * g + 2 * half + 2)
             nc.vector.quantize_mx(
-                out=rt_codes[:, s : s + 2, :, :].rearrange("p s k n -> p (s k n)").bitcast(FP8X4),
-                scales=rt_scales[:, s : s + 2, :, :].rearrange("p s k n -> p (s k n)"),
-                in_=gr[pair][:],
+                out=rd_codes[:, tiles, :, :].rearrange("p s k n -> p (s k n)").bitcast(FP8X4),
+                scales=rd_scales[:, tiles, :, :].rearrange("p s k n -> p (s k n)"),
+                in_=rd_in[g, half][:].rearrange("p s n -> p (s n)"),
             )
 
-        def L(g, k, e):
+        def interleave_rn(g, k, half, copy):
             if g not in rn_in:
-                rn = big.tile([P, 2, 2048], BF16, name="rn", tag="g8", bufs=2, align_bytes=64)
-                rn_in[g] = rn
-            out = rn_in[g][:, k, :].rearrange("p (t m j) -> p t m j", t=4, j=4)
-            in_ = r_in[g][:, :, 512 * k : 512 * (k + 1)].rearrange("p j (m t) -> p t m j", t=4)
-            if e == "g":
-                nc.gpsimd.tensor_scalar(out=out, in0=in_, scalar1=1.0, scalar2=0.0, op0=ALU.mult, op1=ALU.add)
-            else:
-                copy_same(e, out, in_)
+                grouped = work.tile([P, 2, 4 * 512], BF16, name="grouped", tag="grouped", bufs=3, align_bytes=64)
+                rn_in[g] = grouped
+            ts = slice(2 * half, 2 * half + 2)
+            out = rn_in[g][:, k, :].rearrange("p (t m j) -> p t m j", t=4, j=4)[:, ts]
+            in_ = r_in[g][:, :, 512 * k : 512 * (k + 1)].rearrange("p j (m t) -> p t m j", t=4)[:, ts]
+            copy(out=out, in_=in_)
 
-        def Qn(g, k):
+        def copy_on_gpsimd(out, in_):
+            for i in range(2):
+                nc.gpsimd.tensor_scalar(out=out[:, i], in0=in_[:, i], scalar1=1.0, scalar2=0.0, op0=ALU.mult, op1=ALU.add)
+
+        def quantise_rn(g, k):
             nc.vector.quantize_mx(out=rn_codes[:, g, k, :].bitcast(FP8X4), scales=rn_scales[:, g, k, :], in_=rn_in[g][:, k, :])
 
-        def AB():
-            nc.vector.tensor_scalar(out=ab32[:, 0, :], in0=a_in[:], scalar1=2.0, scalar2=None, op0=ALU.mult)
-            nc.vector.tensor_copy(out=ab32[:, 1, :], in_=b_in[:])
+        def labels(g, half):
+            part = u_in[g][:, 2 * half : 2 * half + 2, :]
+            nc.vector.tensor_scalar(out=part, in0=part, scalar1=THRESHOLD, scalar2=0.5, op0=ALU.is_gt, op1=ALU.subtract)
 
-        def S(g, e):
-            eng = nc.vector if e == "v" else nc.gpsimd
-            eng.tensor_scalar(out=u_in[g][:], in0=u_in[g][:], scalar1=0.7, scalar2=0.5, op0=ALU.is_gt, op1=ALU.subtract)
+        def region_constants():
+            nc.vector.tensor_scalar(out=a2[:], in0=a_in[:], scalar1=2.0, scalar2=None, op0=ALU.mult)
+            nc.vector.tensor_copy(out=b1[:], in_=b_in[:])
+            nc.vector.tensor_scalar(out=ah[:], in0=a_in[:], scalar1=-0.5, scalar2=None, op0=ALU.mult)
 
-        def W(g, h, e):
-            wt = big.tile([P, 4, 512], F32, name="wt", tag="ld", bufs=4, align_bytes=64)
-            w_fac[g, h] = wt
-            eng = nc.vector if e == "v" else nc.gpsimd
+        def weights(g, h, engine):
+            tile = work.tile([P, 4, HALF], F32, name="tile", tag="t_or_weight", bufs=4, align_bytes=64)
+            weight[g, h] = tile
             for j in range(4):
-                eng.tensor_scalar(
-                    out=wt[:, j, :], in0=u_in[g][:, j, 512 * h : 512 * (h + 1)],
-                    scalar1=0.25, scalar2=ab32[:, 0, 4 * g + j : 4 * g + j + 1], op0=ALU.subtract, op1=ALU.mult,
+                col = slice(4 * g + j, 4 * g + j + 1)
+                engine.tensor_scalar(
+                    out=tile[:, j, :], in0=u_in[g][:, j, HALF * h : HALF * (h + 1)],
+                    scalar1=a2[:, col], scalar2=ah[:, col], op0=ALU.mult, op1=ALU.add,
                 )
 
-        def M(g, h, j):
-            bank = psum.tile([P, 512], F32, name="bank", tag="bank", bufs=8)
+        def logits(g, h, j):
+            s = 4 * g + j
+            bank = new_bank()
             for k in range(2):
                 nc.tensor.matmul_mx(
                     out=bank[:],
-                    lhsT=rt_codes[:, 4 * g + j, k, :].bitcast(FP8X4), lhsT_scale=rt_scales[:, 4 * g + j, k, :],
-                    rhs=tt_codes[:, h, k, :].bitcast(FP8X4), rhs_scale=tt_scales[:, h, k, :],
+                    lhsT=rd_codes[:, s, k, :].bitcast(FP8X4), lhsT_scale=rd_scales[:, s, k, :],
+                    rhs=td_codes[:, h, k, :].bitcast(FP8X4), rhs_scale=td_scales[:, h, k, :],
                     start=(k == 0), stop=(k == 1),
                 )
-            banks[g, h, j] = bank
+            bank_of[g, h, j] = bank
 
-        def V(g, h, j):
-            s = 4 * g + j
-            v = work.tile([P, 512], F32, name="v", tag="v", bufs=6, align_bytes=64)
+        def shift_and_sign(g, h, j):
+            v = work.tile([P, HALF], F32, name="v", tag="v", bufs=6, align_bytes=64)
             nc.vector.scalar_tensor_tensor(
-                out=v[:], in0=banks[g, h, j][:], scalar=ab32[:, 1, s : s + 1],
-                in1=u_in[g][:, j, 512 * h : 512 * (h + 1)], op0=ALU.add, op1=ALU.mult,
+                out=v[:], in0=bank_of[g, h, j][:], scalar=b1[:, 4 * g + j : 4 * g + j + 1],
+                in1=u_in[g][:, j, HALF * h : HALF * (h + 1)], op0=ALU.add, op1=ALU.mult,
             )
-            vs[g, h, j] = v
+            signed[g, h, j] = v
 
-        def A(g, h, j):
+        def probability(g, h, j):
             if (g, h) not in prob:
-                pt = keep.tile([P, 4, 512], F32, name="prob%d%d" % (g, h), align_bytes=64)
-                prob[g, h] = pt
-            s = 4 * g + j
-            nc.scalar.activation(out=prob[g, h][:, j, :], in_=vs[g, h, j][:], func=ACT.Sigmoid, scale=ab32[:, 0, s : s + 1])
-
-        def where(i):
-            c0, w = BLOCKS[i]
-            return c0 // 512, c0 % 512, w
-
-        def Ln(i, g):
-            h, o, w = where(i)
-            l = work.tile([P, 4, w], F32, name="l", tag="l", bufs=4, align_bytes=64)
-            nc.scalar.activation(out=l[:], in_=prob[g, h][:, :, o : o + w], func=ACT.Ln, bias=2.0 ** -64)
-            lg[i, g] = l
-
-        def Sq(i, g):
-            h, o, w = where(i)
-            q = work.tile([P, 4, w], F32, name="q", tag="q", bufs=3, align_bytes=64)
-            nc.scalar.activation(out=q[:], in_=prob[g, h][:, :, o : o + w], func=ACT.Square, scale=-1.0, bias=1.0)
-            q2[i, g] = q
-
-        def B(i, g):
-            h, o, w = where(i)
-            l = lg[i, g]
-            nc.vector.scalar_tensor_tensor(out=l[:], in0=l[:], scalar=0.5, in1=prob[g, h][:, :, o : o + w], op0=ALU.add, op1=ALU.mult)
-
-        def X(i, g):
-            h, o, w = where(i)
-            l = lg[i, g]
-            nc.vector.scalar_tensor_tensor(out=l[:], in0=l[:], scalar=0.5, in1=w_fac[g, h][:, :, o : o + w], op0=ALU.subtract, op1=ALU.mult)
-
-        def E(i, g):
-            h, o, w = where(i)
-            e = work.tile([P, w, 4], BF16, name="e", tag="e", bufs=3, align_bytes=64)
-            nc.vector.tensor_tensor(
-                out=e[:].rearrange("p (c i) t -> p c t i", i=2),
-                in0=lg[i, g][:].rearrange("p t (c i) -> p c t i", i=2),
-                in1=q2[i, g][:].rearrange("p t (c i) -> p c t i", i=2), op=ALU.mult,
+                prob_tile = keep.tile([P, 4, HALF], F32, name="prob%d%d" % (g, h), align_bytes=64)
+                prob[g, h] = prob_tile
+            nc.scalar.activation(
+                out=prob[g, h][:, j, :], in_=signed[g, h, j][:], func=ACT.Sigmoid, scale=a2[:, 4 * g + j : 4 * g + j + 1]
             )
-            es[i, g] = e
 
-        def Qe(i, g):
-            h, o, w = where(i)
-            codes = work.tile([P, w], U32, name="e_codes", tag="ec", bufs=4, align_bytes=64)
-            scales = work.tile([P, w], U8, name="e_scales", tag="es", bufs=4, align_bytes=64)
-            nc.vector.quantize_mx(out=codes[:].bitcast(FP8X4), scales=scales[:], in_=es[i, g][:].rearrange("p c t -> p (c t)"))
-            ec[i, g] = (codes, scales)
+        def in_block(tiles, i, g):
+            c0, w = BLOCKS[i]
+            return tiles[g, c0 // HALF][:, :, c0 % HALF : c0 % HALF + w]
 
-        def MP(i, ct, k):
-            cs = slice(P * ct, P * (ct + 1))
-            bank = psum.tile([P, 512], F32, name="bank", tag="bank", bufs=8)
+        def logs_and_squares(i):
+            for g in range(2):
+                log_tile = work.tile([P, 4, BLOCKS[i][1]], F32, name="log_tile", tag="log", bufs=4, align_bytes=64)
+                nc.scalar.activation(out=log_tile[:], in_=in_block(prob, i, g), func=ACT.Ln, bias=2.0**-64)
+                log_of[i, g] = log_tile
+            for g in range(2):
+                square = work.tile([P, 4, BLOCKS[i][1]], F32, name="square", tag="square", bufs=4, align_bytes=64)
+                nc.scalar.activation(out=square[:], in_=in_block(prob, i, g), func=ACT.Square, scale=-1.0, bias=1.0)
+                square_of[i, g] = square
+
+        def gradients(i):
+            w = BLOCKS[i][1]
+            for g in range(2):
+                x = log_of[i, g]
+                nc.vector.scalar_tensor_tensor(out=x[:], in0=x[:], scalar=0.5, in1=in_block(prob, i, g), op0=ALU.add, op1=ALU.mult)
+            for g in range(2):
+                x = log_of[i, g]
+                nc.vector.scalar_tensor_tensor(out=x[:], in0=x[:], scalar=0.5, in1=in_block(weight, i, g), op0=ALU.subtract, op1=ALU.mult)
+            for g in range(2):
+                e_tile = work.tile([P, w, 4], BF16, name="e_tile", tag="e", bufs=2, align_bytes=64)
+                nc.vector.tensor_tensor(
+                    out=e_tile[:].rearrange("p (c i) j -> p c j i", i=2),
+                    in0=log_of[i, g][:].rearrange("p j (c i) -> p c j i", i=2),
+                    in1=square_of[i, g][:].rearrange("p j (c i) -> p c j i", i=2), op=ALU.mult,
+                )
+                e_of[i, g] = e_tile
+            for g in range(2):
+                codes = work.tile([P, w], U32, name="codes", tag="e_codes", bufs=4, align_bytes=64)
+                scales = work.tile([P, w], U8, name="scales", tag="e_scales", bufs=4, align_bytes=64)
+                nc.vector.quantize_mx(out=codes[:].bitcast(FP8X4), scales=scales[:], in_=e_of[i, g][:].rearrange("p c j -> p (c j)"))
+                e_codes[i, g] = (codes, scales)
+
+        def plane_products(i, q, k):
+            codes, cols = e_codes, slice(P * q, P * (q + 1))
+            bank = new_bank()
             for j in range(4):
+                part = slice(P * j, P * (j + 1))
                 for g in range(2):
                     nc.tensor.matmul_mx(
-                        out=bank[:, P * j : P * (j + 1)],
-                        lhsT=rn_codes[:, g, k, P * j : P * (j + 1)].bitcast(FP8X4), lhsT_scale=rn_scales[:, g, k, P * j : P * (j + 1)],
-                        rhs=ec[i, g][0][:, cs].bitcast(FP8X4), rhs_scale=ec[i, g][1][:, cs],
+                        out=bank[:, part],
+                        lhsT=rn_codes[:, g, k, part].bitcast(FP8X4), lhsT_scale=rn_scales[:, g, k, part],
+                        rhs=codes[i, g][0][:, cols].bitcast(FP8X4), rhs_scale=codes[i, g][1][:, cols],
                         start=(g == 0), stop=(g == 1),
                     )
-            banks["p", i, ct, k] = bank
+            bank_of["plane", i, q, k] = bank
 
-        def MR(i, ct, k):
-            cs = slice(P * ct, P * (ct + 1))
-            bank = psum.tile([P, 512], F32, name="bank", tag="bank", bufs=8)
+        def row_products(i, q, k):
+            codes, cols = e_codes, slice(P * q, P * (q + 1))
+            bank = new_bank()
             for g in range(2):
                 nc.tensor.matmul_mx(
                     out=bank[:],
-                    lhsT=ec[i, g][0][:, cs].bitcast(FP8X4), lhsT_scale=ec[i, g][1][:, cs],
+                    lhsT=codes[i, g][0][:, cols].bitcast(FP8X4), lhsT_scale=codes[i, g][1][:, cols],
                     rhs=rn_codes[:, g, k, :].bitcast(FP8X4), rhs_scale=rn_scales[:, g, k, :],
                     start=(g == 0), stop=(g == 1),
                 )
-            banks["r", i, ct, k] = bank
+            bank_of["rows", i, q, k] = bank
 
-        def copy_eighth(eng, out, in_):
-            if eng == "s":
-                nc.scalar.mul(out=out, in_=in_, mul=0.125)
-            else:
-                nc.vector.tensor_scalar(out=out, in0=in_, scalar1=0.125, scalar2=None, op0=ALU.mult)
+        def eighth_on_scalar(out, in_):
+            nc.scalar.activation(out=out, in_=in_, func=ACT.Copy, scale=0.125)
 
-        def OP(i, ct, k, e):
-            h, o, w = where(i)
-            if (i, k) not in pb:
-                pbt = work.tile([P, w * 4], BF16, name="pbt", tag="pb", bufs=4, align_bytes=64)
-                pb[i, k] = pbt
-            copy_eighth(
-                e, pb[i, k][:, 512 * ct : 512 * (ct + 1)].rearrange("p (c t) -> p c t", t=4),
-                banks["p", i, ct, k][:].rearrange("p (t c) -> p c t", t=4),
+        def eighth_on_vector(out, in_):
+            nc.vector.tensor_scalar(out=out, in0=in_, scalar1=0.125, scalar2=None, op0=ALU.mult)
+
+        def plane_out(i, q, k, eighth):
+            if (i, k) not in plane_in:
+                plane = work.tile([P, 4 * BLOCKS[i][1]], BF16, name="plane", tag="plane", bufs=4, align_bytes=64)
+                plane_in[i, k] = plane
+            eighth(
+                out=plane_in[i, k][:, BANK * q : BANK * (q + 1)].rearrange("p (c t) -> p c t", t=4),
+                in_=bank_of["plane", i, q, k][:].rearrange("p (t c) -> p c t", t=4),
             )
 
-        def OR(i, ct, k, e):
-            c0 = BLOCKS[i][0]
-            if (i, ct) not in ro:
-                rot = work.tile([P, 1024], F32, name="rot", tag="ro", bufs=3, align_bytes=64)
-                ro[i, ct] = rot
-            copy_eighth(
-                e, ro[i, ct][:, 512 * k : 512 * (k + 1)].rearrange("p (m t) -> p m t", t=4),
-                banks["r", i, ct, k][:].rearrange("p (t m) -> p m t", t=4),
+        def row_out(i, q, k, eighth):
+            c0 = BLOCKS[i][0] + P * q
+            last = i == len(BLOCKS) - 1
+            if (i, q) not in rows_out:
+                rows = work.tile([P, D], F32, name="rows", tag="rows", bufs=2, align_bytes=64)
+                rows_out[i, q] = rows
+            eighth(
+                out=rows_out[i, q][:, BANK * k : BANK * (k + 1)].rearrange("p (m t) -> p m t", t=4),
+                in_=bank_of["rows", i, q, k][:].rearrange("p (t m) -> p m t", t=4),
             )
-            if k == 1:
-                nc.sync.dma_start(out=out_0[c0 + P * ct : c0 + P * (ct + 1), :], in_=ro[i, ct][:])
+            if last or k == 1:
+                cols = slice(BANK * k, BANK * (k + 1)) if last else slice(0, D)
+                nc.sync.dma_start(out=out_0[c0 : c0 + P, cols], in_=rows_out[i, q][:, cols])
 
-        def QP(i, k):
+        def quantise_plane(i, k):
             c0, w = BLOCKS[i]
-            pc = work.tile([P, w], U32, name="pc", tag="pc", bufs=4, align_bytes=64)
-            nc.vector.quantize_mx(out=pc[:].bitcast(FP8X4), scales=p_scales[:, k, c0 : c0 + w], in_=pb[i, k][:])
-            nc.sync.dma_start(out=out_1[k, :, c0 : c0 + w, :].rearrange("p m t -> p (m t)").bitcast(I32), in_=pc[:].bitcast(I32))
+            words = work.tile([P, w], U32, name="words", tag="words", bufs=4, align_bytes=64)
+            nc.vector.quantize_mx(out=words[:].bitcast(FP8X4), scales=out_scales[:, k, c0 : c0 + w], in_=plane_in[i, k][:])
+            nc.sync.dma_start(out=out_1[k, :, c0 : c0 + w, :].rearrange("p m t -> p (m t)").bitcast(I32), in_=words[:].bitcast(I32))
 
-        def SC(c0, c1):
+        def store_scales(c0, c1):
             for q in range(4):
                 nc.sync.dma_start(
-                    out=out_2[:, 4 * q : 4 * q + 4, c0:c1].bitcast(I32).rearrange("k r c -> r k c"),
-                    in_=p_scales[32 * q : 32 * q + 4, :, c0:c1].bitcast(I32),
+                    out=out_2[:, 4 * q : 4 * q + 4, c0:c1].bitcast(I32).rearrange("k x c -> x k c"),
+                    in_=out_scales[32 * q : 32 * q + 4, :, c0:c1].bitcast(I32),
                 )
 
-        steps = {
-            "D": D,
-            "Tt": Tt, "Qt": Qt, "Tr": Tr, "Qr": Qr, "L": L, "Qn": Qn, "AB": AB, "S": S, "W": W, "M": M, "V": V, "A": A,
-            "Ln": Ln, "Sq": Sq, "B": B, "X": X, "E": E, "Qe": Qe, "MP": MP, "MR": MR, "OP": OP, "OR": OR, "QP": QP, "SC": SC,
-        }
+        on_scalar = nc.scalar.copy
+        on_vector = nc.vector.tensor_copy
 
-        def run(text):
-            for item in text.split():
-                parts = item.split(",")
-                steps[parts[0]](*[x if x in "svg" else int(x) for x in parts[1:]])
+        labels(0, 0)
+        warm_up(new_bank(), 13)
+        region_constants()
+        turn_t(0, 0, on_vector)
+        turn_t(0, 1, on_vector)
+        turn_t(0, 2, on_scalar)
+        turn_t(0, 3, on_scalar, dummies=2)
+        labels(0, 1)
+        weights(0, 0, nc.vector)
+        turn_r(0, 0, on_scalar)
+        interleave_rn(0, 0, 0, on_scalar)
+        turn_r(0, 1, on_scalar)
+        quantise_td(0, 0)
+        interleave_rn(0, 1, 0, on_vector)
+        quantise_td(0, 1)
+        turn_r(0, 2, on_scalar, dummies=2)
+        turn_r(0, 3, on_scalar)
+        quantise_rd(0, 0)
+        interleave_rn(0, 1, 1, on_vector)
+        quantise_rd(0, 1)
 
-        run(HEAD)
-        run(TAIL)
+        turn_t(1, 0, on_scalar)
+        turn_t(1, 1, on_scalar, dummies=2)
+        turn_t(1, 2, on_scalar)
+        interleave_rn(1, 0, 0, on_scalar)
+        interleave_rn(0, 0, 1, on_scalar)
+        turn_t(1, 3, on_vector)
+        turn_r(1, 0, on_vector)
+        for j in range(2):
+            logits(0, 0, j)
+        for j in range(2):
+            shift_and_sign(0, 0, j)
+        for j in range(1, 4):
+            turn_r(1, j, on_scalar)
+        for k in range(2):
+            quantise_td(1, k)
+        quantise_rd(1, 0)
+        labels(1, 0)
+        quantise_rd(1, 1)
+        for h, j in ((0, 2), (0, 3), (1, 0), (1, 1)):
+            logits(0, h, j)
+        probability(0, 0, 0)
+        interleave_rn(1, 0, 1, on_scalar)
+        probability(0, 0, 1)
+        shift_and_sign(0, 0, 2)
+        labels(1, 1)
+        shift_and_sign(0, 0, 3)
+        for j in range(2, 4):
+            probability(0, 0, j)
+        weights(0, 1, nc.gpsimd)
+        interleave_rn(1, 1, 1, copy_on_gpsimd)
+        for j in range(2, 4):
+            logits(0, 1, j)
+
+        for g, h in ((0, 1), (1, 0), (1, 1)):
+            if g == 1:
+                for j in range(4):
+                    logits(g, h, j)
+            for j in range(4):
+                shift_and_sign(g, h, j)
+            for j in range(4):
+                probability(g, h, j)
+            if h == 1 and g == 0:
+                weights(1, 0, nc.gpsimd)
+            if h == 0:
+                interleave_rn(1, 1, 0, copy_on_gpsimd)
+                weights(1, 1, nc.gpsimd)
+        for g in range(2):
+            for k in range(2):
+                quantise_rn(g, k)
+
+        last = len(BLOCKS) - 1
+        logs_and_squares(0)
+        for i in range(last + 1):
+            if i < last:
+                logs_and_squares(i + 1)
+            gradients(i)
+            if i > 0:
+                for q in range(BLOCKS[i - 1][1] // P):
+                    for k in range(2):
+                        plane_out(i - 1, q, k, eighth_on_vector if (i - 1, q, k) == (0, 1, 1) else eighth_on_scalar)
+                    for k in range(2):
+                        row_out(i - 1, q, k, eighth_on_scalar)
+                for k in range(2):
+                    quantise_plane(i - 1, k)
+                if i == last - 1:
+                    store_scales(0, BLOCKS[i][0])
+            if i < last:
+                for q in range(BLOCKS[i][1] // P):
+                    for k in range(2):
+                        plane_products(i, q, k)
+                    for k in range(2):
+                        row_products(i, q, k)
+
+        for k in range(2):
+            row_products(last, 0, k)
+        for k in range(2):
+            plane_products(last, 0, k)
+        for k in range(2):
+            row_out(last, 0, k, (eighth_on_scalar, eighth_on_vector)[k])
+        for k in range(2):
+            plane_out(last, 0, k, (eighth_on_scalar, eighth_on_vector)[k])
+        for k in range(2):
+            quantise_plane(last, k)
+        store_scales(BLOCKS[last - 1][0], C)

from contextlib import ExitStack

import concourse.mybir as mybir
from concourse.masks import make_identity

N, D, C = 1024, 1024, 1024
FLOPS = 2 * (2 * N * D * C)

F32 = mybir.dt.float32
BF16 = mybir.dt.bfloat16
U32 = mybir.dt.uint32
I32 = mybir.dt.int32
U8 = mybir.dt.uint8
FP8X4 = mybir.dt.float8_e4m3fn_x4
ALU = mybir.AluOpType
ACT = mybir.ActivationFunctionType

P = 128
BANK = 512
HALF = 512
THRESHOLD = 0.7

BLOCKS = ((0, 256), (256, 256), (512, 256), (768, 128), (896, 128))


def tile_owlshiftscalefocaltextgradient_x1_kernel(tc, r, t, a, b, u, out_0, out_1, out_2):
    nc = tc.nc
    with ExitStack() as ctx:
        keep = ctx.enter_context(tc.tile_pool(name="keep", bufs=1))
        work = ctx.enter_context(tc.tile_pool(name="work", bufs=4))
        psum = ctx.enter_context(tc.psum_pool(name="psum", bufs=8))
        ctx.enter_context(tc.manual_schedule())

        a_in = keep.tile([P, 8], BF16, name="a_in", align_bytes=64)
        b_in = keep.tile([P, 8], BF16, name="b_in", align_bytes=64)
        for vec, dst in ((a, a_in), (b, b_in)):
            nc.scalar.dma_start(out=dst[:].rearrange("p (g j) -> p g j", j=4), in_=vec.rearrange("(g p j) -> p g j", p=P, j=4))

        t_in = [work.tile([P, 4, D], BF16, name="t_in", tag="t_or_weight", bufs=4, align_bytes=64) for h in range(2)]
        r_in = [keep.tile([P, 4, D], BF16, name="r_in%d" % g, align_bytes=64) for g in range(2)]
        u_in = [keep.tile([P, 4, C], BF16, name="u_in%d" % g, align_bytes=64) for g in range(2)]

        def load_t(h, i, n):
            rows = t[HALF * h : HALF * (h + 1), :].rearrange("(i p) d -> p i d", p=P)
            nc.sync.dma_start(out=t_in[h][:, i : i + n, :], in_=rows[:, i : i + n, :])

        def load_regions(dst, src, g, j, n):
            rows = src[512 * g : 512 * (g + 1), :].rearrange("(p j) c -> p j c", j=4)
            nc.sync.dma_start(out=dst[g][:, j : j + n, :], in_=rows[:, j : j + n, :])

        load_t(0, 0, 2)
        load_regions(u_in, u, 0, 0, 2)
        load_t(0, 2, 1)
        load_t(0, 3, 1)
        load_regions(u_in, u, 0, 2, 2)
        load_regions(r_in, r, 0, 0, 2)
        load_regions(r_in, r, 0, 2, 2)
        load_t(1, 0, 2)
        load_t(1, 2, 2)
        load_regions(r_in, r, 1, 0, 2)
        load_regions(r_in, r, 1, 2, 2)
        load_regions(u_in, u, 1, 0, 4)

        ident = keep.tile([P, P], F32, name="ident", align_bytes=64)
        make_identity(nc, ident[:])
        table_warm_up = keep.tile([P, 1], F32, name="table_warm_up")
        nc.scalar.activation(out=table_warm_up[:], in_=ident[:, 0:1], func=ACT.Sigmoid)
        zeros = keep.tile([P, BANK], BF16, name="zeros", align_bytes=64)
        nc.vector.memset(zeros[:], 0.0)

        a2 = keep.tile([P, 8], F32, name="a2", align_bytes=64)
        b1 = keep.tile([P, 8], F32, name="b1", align_bytes=64)
        ah = keep.tile([P, 8], F32, name="ah", align_bytes=64)

        rd_codes = keep.tile([P, 8, 2, P], U32, name="rd_codes", align_bytes=64)
        rd_scales = keep.tile([P, 8, 2, P], U8, name="rd_scales", align_bytes=64)
        td_codes = keep.tile([P, 2, 2, HALF], U32, name="td_codes", align_bytes=64)
        td_scales = keep.tile([P, 2, 2, HALF], U8, name="td_scales", align_bytes=64)
        rn_codes = keep.tile([P, 2, 2, 512], U32, name="rn_codes", align_bytes=64)
        rn_scales = keep.tile([P, 2, 2, 512], U8, name="rn_scales", align_bytes=64)
        out_scales = keep.tile([P, 2, C], U8, name="out_scales", align_bytes=64)

        td_in = {}
        rd_in = {}
        rn_in = {}
        weight = {}
        prob = {}
        bank_of = {}
        signed = {}
        log_of = {}
        square_of = {}
        e_of = {}
        e_codes = {}
        plane_in = {}
        rows_out = {}

        def new_bank():
            bank = psum.tile([P, BANK], F32, name="bank", tag="bank", bufs=8)
            return bank

        def warm_up(bank, n):
            for i in range(n):
                nc.tensor.matmul(bank[:], lhsT=zeros[:, 0:P], rhs=zeros[:], start=True, stop=True)

        def turn(rows, copy, out, dummies):
            words = rows.bitcast(F32)
            bank = new_bank()
            warm_up(bank, dummies)
            turned = bank[:].rearrange("p (k w n) -> p k w n", k=2, w=2)
            for k in range(2):
                for w in range(2):
                    nc.tensor.transpose(turned[:, k, w, :], words[:, 256 * k + w : 256 * (k + 1) : 2], ident[:])
            copy(out=out, in_=turned.rearrange("p k w n -> p k n w"))

        def turn_t(h, i, copy, dummies=0):
            if h not in td_in:
                grouped = work.tile([P, 2, 4 * HALF], BF16, name="grouped", tag="grouped", bufs=3, align_bytes=64)
                td_in[h] = grouped
            out = td_in[h][:, :, 512 * i : 512 * (i + 1)].bitcast(F32).rearrange("p k (n w) -> p k n w", w=2)
            turn(t_in[h][:, i, :], copy, out, dummies)

        def turn_r(g, j, copy, dummies=0):
            pair = (g, j // 2)
            if pair not in rd_in:
                pair_in = work.tile([P, 2, 4 * 2 * P], BF16, name="pair_in", tag="pair_in", bufs=2, align_bytes=64)
                rd_in[pair] = pair_in
            out = rd_in[pair][:, j % 2, :].bitcast(F32).rearrange("p (k n w) -> p k n w", k=2, w=2)
            turn(r_in[g][:, j, :], copy, out, dummies)

        def quantise_td(h, k):
            nc.vector.quantize_mx(out=td_codes[:, h, k, :].bitcast(FP8X4), scales=td_scales[:, h, k, :], in_=td_in[h][:, k, :])

        def quantise_rd(g, half):
            tiles = slice(4 * g + 2 * half, 4 * g + 2 * half + 2)
            nc.vector.quantize_mx(
                out=rd_codes[:, tiles, :, :].rearrange("p s k n -> p (s k n)").bitcast(FP8X4),
                scales=rd_scales[:, tiles, :, :].rearrange("p s k n -> p (s k n)"),
                in_=rd_in[g, half][:].rearrange("p s n -> p (s n)"),
            )

        def interleave_rn(g, k, half, copy):
            if g not in rn_in:
                grouped = work.tile([P, 2, 4 * 512], BF16, name="grouped", tag="grouped", bufs=3, align_bytes=64)
                rn_in[g] = grouped
            ts = slice(2 * half, 2 * half + 2)
            out = rn_in[g][:, k, :].rearrange("p (t m j) -> p t m j", t=4, j=4)[:, ts]
            in_ = r_in[g][:, :, 512 * k : 512 * (k + 1)].rearrange("p j (m t) -> p t m j", t=4)[:, ts]
            copy(out=out, in_=in_)

        def copy_on_gpsimd(out, in_):
            for i in range(2):
                nc.gpsimd.tensor_scalar(out=out[:, i], in0=in_[:, i], scalar1=1.0, scalar2=0.0, op0=ALU.mult, op1=ALU.add)

        def quantise_rn(g, k):
            nc.vector.quantize_mx(out=rn_codes[:, g, k, :].bitcast(FP8X4), scales=rn_scales[:, g, k, :], in_=rn_in[g][:, k, :])

        def labels(g, half):
            part = u_in[g][:, 2 * half : 2 * half + 2, :]
            nc.vector.tensor_scalar(out=part, in0=part, scalar1=THRESHOLD, scalar2=0.5, op0=ALU.is_gt, op1=ALU.subtract)

        def region_constants():
            nc.vector.tensor_scalar(out=a2[:], in0=a_in[:], scalar1=2.0, scalar2=None, op0=ALU.mult)
            nc.vector.tensor_copy(out=b1[:], in_=b_in[:])
            nc.vector.tensor_scalar(out=ah[:], in0=a_in[:], scalar1=-0.5, scalar2=None, op0=ALU.mult)

        def weights(g, h, engine):
            tile = work.tile([P, 4, HALF], F32, name="tile", tag="t_or_weight", bufs=4, align_bytes=64)
            weight[g, h] = tile
            for j in range(4):
                col = slice(4 * g + j, 4 * g + j + 1)
                engine.tensor_scalar(
                    out=tile[:, j, :], in0=u_in[g][:, j, HALF * h : HALF * (h + 1)],
                    scalar1=a2[:, col], scalar2=ah[:, col], op0=ALU.mult, op1=ALU.add,
                )

        def logits(g, h, j):
            s = 4 * g + j
            bank = new_bank()
            for k in range(2):
                nc.tensor.matmul_mx(
                    out=bank[:],
                    lhsT=rd_codes[:, s, k, :].bitcast(FP8X4), lhsT_scale=rd_scales[:, s, k, :],
                    rhs=td_codes[:, h, k, :].bitcast(FP8X4), rhs_scale=td_scales[:, h, k, :],
                    start=(k == 0), stop=(k == 1),
                )
            bank_of[g, h, j] = bank

        def shift_and_sign(g, h, j):
            v = work.tile([P, HALF], F32, name="v", tag="v", bufs=6, align_bytes=64)
            nc.vector.scalar_tensor_tensor(
                out=v[:], in0=bank_of[g, h, j][:], scalar=b1[:, 4 * g + j : 4 * g + j + 1],
                in1=u_in[g][:, j, HALF * h : HALF * (h + 1)], op0=ALU.add, op1=ALU.mult,
            )
            signed[g, h, j] = v

        def probability(g, h, j):
            if (g, h) not in prob:
                prob_tile = keep.tile([P, 4, HALF], F32, name="prob%d%d" % (g, h), align_bytes=64)
                prob[g, h] = prob_tile
            nc.scalar.activation(
                out=prob[g, h][:, j, :], in_=signed[g, h, j][:], func=ACT.Sigmoid, scale=a2[:, 4 * g + j : 4 * g + j + 1]
            )

        def in_block(tiles, i, g):
            c0, w = BLOCKS[i]
            return tiles[g, c0 // HALF][:, :, c0 % HALF : c0 % HALF + w]

        def logs_and_squares(i):
            for g in range(2):
                log_tile = work.tile([P, 4, BLOCKS[i][1]], F32, name="log_tile", tag="log", bufs=4, align_bytes=64)
                nc.scalar.activation(out=log_tile[:], in_=in_block(prob, i, g), func=ACT.Ln, bias=2.0**-64)
                log_of[i, g] = log_tile
            for g in range(2):
                square = work.tile([P, 4, BLOCKS[i][1]], F32, name="square", tag="square", bufs=4, align_bytes=64)
                nc.scalar.activation(out=square[:], in_=in_block(prob, i, g), func=ACT.Square, scale=-1.0, bias=1.0)
                square_of[i, g] = square

        def gradients(i):
            w = BLOCKS[i][1]
            for g in range(2):
                x = log_of[i, g]
                nc.vector.scalar_tensor_tensor(out=x[:], in0=x[:], scalar=0.5, in1=in_block(prob, i, g), op0=ALU.add, op1=ALU.mult)
            for g in range(2):
                x = log_of[i, g]
                nc.vector.scalar_tensor_tensor(out=x[:], in0=x[:], scalar=0.5, in1=in_block(weight, i, g), op0=ALU.subtract, op1=ALU.mult)
            for g in range(2):
                e_tile = work.tile([P, w, 4], BF16, name="e_tile", tag="e", bufs=2, align_bytes=64)
                nc.vector.tensor_tensor(
                    out=e_tile[:].rearrange("p (c i) j -> p c j i", i=2),
                    in0=log_of[i, g][:].rearrange("p j (c i) -> p c j i", i=2),
                    in1=square_of[i, g][:].rearrange("p j (c i) -> p c j i", i=2), op=ALU.mult,
                )
                e_of[i, g] = e_tile
            for g in range(2):
                codes = work.tile([P, w], U32, name="codes", tag="e_codes", bufs=4, align_bytes=64)
                scales = work.tile([P, w], U8, name="scales", tag="e_scales", bufs=4, align_bytes=64)
                nc.vector.quantize_mx(out=codes[:].bitcast(FP8X4), scales=scales[:], in_=e_of[i, g][:].rearrange("p c j -> p (c j)"))
                e_codes[i, g] = (codes, scales)

        def plane_products(i, q, k):
            codes, cols = e_codes, slice(P * q, P * (q + 1))
            bank = new_bank()
            for j in range(4):
                part = slice(P * j, P * (j + 1))
                for g in range(2):
                    nc.tensor.matmul_mx(
                        out=bank[:, part],
                        lhsT=rn_codes[:, g, k, part].bitcast(FP8X4), lhsT_scale=rn_scales[:, g, k, part],
                        rhs=codes[i, g][0][:, cols].bitcast(FP8X4), rhs_scale=codes[i, g][1][:, cols],
                        start=(g == 0), stop=(g == 1),
                    )
            bank_of["plane", i, q, k] = bank

        def row_products(i, q, k):
            codes, cols = e_codes, slice(P * q, P * (q + 1))
            bank = new_bank()
            for g in range(2):
                nc.tensor.matmul_mx(
                    out=bank[:],
                    lhsT=codes[i, g][0][:, cols].bitcast(FP8X4), lhsT_scale=codes[i, g][1][:, cols],
                    rhs=rn_codes[:, g, k, :].bitcast(FP8X4), rhs_scale=rn_scales[:, g, k, :],
                    start=(g == 0), stop=(g == 1),
                )
            bank_of["rows", i, q, k] = bank

        def eighth_on_scalar(out, in_):
            nc.scalar.activation(out=out, in_=in_, func=ACT.Copy, scale=0.125)

        def eighth_on_vector(out, in_):
            nc.vector.tensor_scalar(out=out, in0=in_, scalar1=0.125, scalar2=None, op0=ALU.mult)

        def plane_out(i, q, k, eighth):
            if (i, k) not in plane_in:
                plane = work.tile([P, 4 * BLOCKS[i][1]], BF16, name="plane", tag="plane", bufs=4, align_bytes=64)
                plane_in[i, k] = plane
            eighth(
                out=plane_in[i, k][:, BANK * q : BANK * (q + 1)].rearrange("p (c t) -> p c t", t=4),
                in_=bank_of["plane", i, q, k][:].rearrange("p (t c) -> p c t", t=4),
            )

        def row_out(i, q, k, eighth):
            c0 = BLOCKS[i][0] + P * q
            last = i == len(BLOCKS) - 1
            if (i, q) not in rows_out:
                rows = work.tile([P, D], F32, name="rows", tag="rows", bufs=2, align_bytes=64)
                rows_out[i, q] = rows
            eighth(
                out=rows_out[i, q][:, BANK * k : BANK * (k + 1)].rearrange("p (m t) -> p m t", t=4),
                in_=bank_of["rows", i, q, k][:].rearrange("p (t m) -> p m t", t=4),
            )
            if last or k == 1:
                cols = slice(BANK * k, BANK * (k + 1)) if last else slice(0, D)
                nc.sync.dma_start(out=out_0[c0 : c0 + P, cols], in_=rows_out[i, q][:, cols])

        def quantise_plane(i, k):
            c0, w = BLOCKS[i]
            words = work.tile([P, w], U32, name="words", tag="words", bufs=4, align_bytes=64)
            nc.vector.quantize_mx(out=words[:].bitcast(FP8X4), scales=out_scales[:, k, c0 : c0 + w], in_=plane_in[i, k][:])
            nc.sync.dma_start(out=out_1[k, :, c0 : c0 + w, :].rearrange("p m t -> p (m t)").bitcast(I32), in_=words[:].bitcast(I32))

        def store_scales(c0, c1):
            for q in range(4):
                nc.sync.dma_start(
                    out=out_2[:, 4 * q : 4 * q + 4, c0:c1].bitcast(I32).rearrange("k x c -> x k c"),
                    in_=out_scales[32 * q : 32 * q + 4, :, c0:c1].bitcast(I32),
                )

        on_scalar = nc.scalar.copy
        on_vector = nc.vector.tensor_copy

        labels(0, 0)
        warm_up(new_bank(), 13)
        region_constants()
        turn_t(0, 0, on_vector)
        turn_t(0, 1, on_vector)
        turn_t(0, 2, on_scalar)
        turn_t(0, 3, on_scalar, dummies=2)
        labels(0, 1)
        weights(0, 0, nc.vector)
        turn_r(0, 0, on_scalar)
        interleave_rn(0, 0, 0, on_scalar)
        turn_r(0, 1, on_scalar)
        quantise_td(0, 0)
        interleave_rn(0, 1, 0, on_vector)
        quantise_td(0, 1)
        turn_r(0, 2, on_scalar, dummies=2)
        turn_r(0, 3, on_scalar)
        quantise_rd(0, 0)
        interleave_rn(0, 1, 1, on_vector)
        quantise_rd(0, 1)

        turn_t(1, 0, on_scalar)
        turn_t(1, 1, on_scalar, dummies=2)
        turn_t(1, 2, on_scalar)
        interleave_rn(1, 0, 0, on_scalar)
        interleave_rn(0, 0, 1, on_scalar)
        turn_t(1, 3, on_vector)
        turn_r(1, 0, on_vector)
        for j in range(2):
            logits(0, 0, j)
        for j in range(2):
            shift_and_sign(0, 0, j)
        for j in range(1, 4):
            turn_r(1, j, on_scalar)
        for k in range(2):
            quantise_td(1, k)
        quantise_rd(1, 0)
        labels(1, 0)
        quantise_rd(1, 1)
        for h, j in ((0, 2), (0, 3), (1, 0), (1, 1)):
            logits(0, h, j)
        probability(0, 0, 0)
        interleave_rn(1, 0, 1, on_scalar)
        probability(0, 0, 1)
        shift_and_sign(0, 0, 2)
        labels(1, 1)
        shift_and_sign(0, 0, 3)
        for j in range(2, 4):
            probability(0, 0, j)
        weights(0, 1, nc.gpsimd)
        interleave_rn(1, 1, 1, copy_on_gpsimd)
        for j in range(2, 4):
            logits(0, 1, j)

        for g, h in ((0, 1), (1, 0), (1, 1)):
            if g == 1:
                for j in range(4):
                    logits(g, h, j)
            for j in range(4):
                shift_and_sign(g, h, j)
            for j in range(4):
                probability(g, h, j)
            if h == 1 and g == 0:
                weights(1, 0, nc.gpsimd)
            if h == 0:
                interleave_rn(1, 1, 0, copy_on_gpsimd)
                weights(1, 1, nc.gpsimd)
        for g in range(2):
            for k in range(2):
                quantise_rn(g, k)

        last = len(BLOCKS) - 1
        logs_and_squares(0)
        for i in range(last + 1):
            if i < last:
                logs_and_squares(i + 1)
            gradients(i)
            if i > 0:
                for q in range(BLOCKS[i - 1][1] // P):
                    for k in range(2):
                        plane_out(i - 1, q, k, eighth_on_vector if (i - 1, q, k) == (0, 1, 1) else eighth_on_scalar)
                    for k in range(2):
                        row_out(i - 1, q, k, eighth_on_scalar)
                for k in range(2):
                    quantise_plane(i - 1, k)
                if i == last - 1:
                    store_scales(0, BLOCKS[i][0])
            if i < last:
                for q in range(BLOCKS[i][1] // P):
                    for k in range(2):
                        plane_products(i, q, k)
                    for k in range(2):
                        row_products(i, q, k)

        for k in range(2):
            row_products(last, 0, k)
        for k in range(2):
            plane_products(last, 0, k)
        for k in range(2):
            row_out(last, 0, k, (eighth_on_scalar, eighth_on_vector)[k])
        for k in range(2):
            plane_out(last, 0, k, (eighth_on_scalar, eighth_on_vector)[k])
        for k in range(2):
            quantise_plane(last, k)
        store_scales(BLOCKS[last - 1][0], C)
